import numpy as np
import ml_dtypes


def mxq(x, axis, fmt="e4m3"):
    dtype, down = {"e4m3": (ml_dtypes.float8_e4m3fn, 7), "e5m2": (ml_dtypes.float8_e5m2, 14)}[fmt]
    v = np.moveaxis(np.asarray(x, np.float32).astype(ml_dtypes.bfloat16).astype(np.float64), axis, -1)
    blocks = v.reshape(v.shape[:-1] + (-1, 32))
    amax = np.abs(blocks).max(-1, keepdims=True)
    byte = np.maximum(np.where(amax > 0, np.frexp(amax)[1] - 1 + 127, 0) - down, 1)
    scale = np.exp2(byte - 127.0)
    codes = (blocks / scale).astype(np.float32).astype(dtype).astype(np.float64)
    return np.moveaxis((codes * scale).reshape(v.shape), -1, axis)


WIDE = False


def mx_kscale(k):
    if not WIDE:
        return np.ones(k)
    levels = np.array([10, -10, 5, -5, 0])
    if k % 512:
        return np.exp2(np.random.permutation(np.resize(levels, k // 32))).repeat(32)
    a = np.empty((k // 512, 16))
    for p in range(k // 512):
        a[p, :8] = np.random.permutation(np.resize(levels, 8))
        for g in range(8):
            far = levels[np.abs(levels - a[p, g]) >= 10]
            a[p, g + 8] = far[np.random.randint(len(far))]
    return np.exp2(a.ravel()).repeat(32)


BF16 = ml_dtypes.bfloat16


def bf(x):
    return np.asarray(x, np.float32).astype(BF16)


def f64(x):
    return np.asarray(x).astype(np.float64)


T, N, D, F, R, K = 4, 512, 512, 512, 512, 3


def softmax(v):
    e = np.exp(v - v.max(-1, keepdims=True))
    return e / e.sum(-1, keepdims=True)


def transitions(edge, e1, e2):
    lg = np.maximum(mxq(e1, 1, "e4m3") @ mxq(e2, 1, "e4m3").T, 0.0)
    forward = softmax(edge)
    backward = softmax(edge.T)
    adaptive = softmax(lg)
    return np.stack([forward, backward, adaptive], axis=0)


def draw0():
    s, t, r = mx_kscale(D), mx_kscale(N), mx_kscale(R)
    c = np.sqrt(2.0) / R**0.25
    return {"x": bf(np.random.standard_normal((T, N, D)) * s / t[:, None]),
            "edge": bf(np.random.standard_normal((N, N)) * 2.0),
            "e1": bf(np.random.standard_normal((N, R)) * c * r),
            "e2": bf(np.random.standard_normal((N, R)) * c / r),
            "w": bf(np.random.standard_normal((K, D, F)) / np.sqrt(D) / s[:, None]),
            "g": bf(np.random.standard_normal((K, N)) * 2.0 * t),
            "bias": bf(np.random.standard_normal(F) * 0.4)}


def core(x, edge, e1, e2, w, g, bias):
    p = transitions(f64(edge), f64(e1), f64(e2))
    q = p * f64(g)[:, None, :]
    h = mxq(f64(x), 2, "e4m3")[None] @ mxq(f64(w), 1, "e4m3")[:, None]
    z = mxq(q, 2, "e4m3")[:, None] @ mxq(h, 2, "e4m3")
    y = z[0] + z[1] + z[2] + f64(bias)
    return np.maximum(y, 0.0)


def e4m3fn_bytes(y):
    return np.clip(np.asarray(y, np.float64), -448.0, 448.0).astype(np.float32).astype(ml_dtypes.float8_e4m3fn).view(np.uint8)


def e4m3fn_values(b):
    return np.asarray(b, np.uint8).view(ml_dtypes.float8_e4m3fn).astype(np.float64)


def setup_inputs():
    d = draw0()
    x0 = np.asarray(d['w']).astype(np.float64)
    s = (np.max(np.abs(x0), axis=(0, 2), keepdims=True) / 448.0).astype(np.float32)
    out = {}
    for k, v in d.items():
        if k == 'w':
            out['w_bytes'] = e4m3fn_bytes(x0 / s.astype(np.float64))
            out['w_scale'] = s
        else:
            out[k] = v
    return out


def reference(x, edge, e1, e2, w_bytes, w_scale, g, bias):
    return core(x, edge, e1, e2, e4m3fn_values(w_bytes) * w_scale.astype(np.float64), g, bias)

@@ -1,0 +1,497 @@
+from contextlib import ExitStack
+
+import concourse.mybir as mybir
+from concourse.masks import make_identity
+
+T, N, D, F, R, K = 4, 512, 512, 512, 512, 3
+FLOPS = 2 * N * N * R + 2 * K * T * N * D * F + 2 * K * T * N * N * F
+
+P = 128
+PACK = 4
+C = 4
+
+F32 = mybir.dt.float32
+BF16 = mybir.dt.bfloat16
+U32 = mybir.dt.uint32
+U8 = mybir.dt.uint8
+FP8 = mybir.dt.float8_e4m3fn
+FP8X4 = mybir.dt.float8_e4m3fn_x4
+ALU = mybir.AluOpType
+ACT = mybir.ActivationFunctionType
+AX = mybir.AxisListType
+
+
+def tile_graphwavenetdiffusionconv_kernel(tc, x, edge, e1, e2, w_bytes, w_scale, g, bias, out):
+    nc = tc.nc
+    with ExitStack() as ctx:
+        const = ctx.enter_context(tc.tile_pool(name="const", bufs=1))
+        work = ctx.enter_context(tc.tile_pool(name="work", bufs=2))
+        ps_h = ctx.enter_context(tc.psum_pool(name="ps_h", bufs=2))
+        ps_t = ctx.enter_context(tc.psum_pool(name="ps_t", bufs=2))
+        ps_z = ctx.enter_context(tc.psum_pool(name="ps_z", bufs=4))
+        ctx.enter_context(tc.manual_schedule())
+
+        rows = const.tile([P, 4 * 512], BF16, name="rows")
+        ones = const.tile([P, P], BF16, name="ones")
+        dummy = const.tile([P, 1], F32, name="dummy")
+        nc.vector.memset(rows[:].bitcast(U32), 0)
+        nc.vector.memset(ones[:], 1.0)
+        nc.gpsimd.memset(dummy[:], 0.0)
+        ws = const.tile([P, PACK], F32, name="ws")
+        wb = [const.tile([P, PACK, F], U8, name=f"wb{k}") for k in range(K)]
+        xs = [const.tile([P, PACK, D], BF16, name=f"x{t}") for t in range(T)]
+        ed = const.tile([P, C, N], BF16, name="ed")
+        es = [const.tile([P, C, R], BF16, name=f"e{i}") for i in range(2)]
+
+        def load_w(k):
+            nc.sync.dma_start(out=wb[k][:], in_=w_bytes[k].rearrange("(p t) f -> p t f", t=PACK))
+
+        def load_x(t):
+            nc.sync.dma_start(out=xs[t][:], in_=x[t].rearrange("(m s) d -> m s d", s=PACK))
+
+        nc.sync.dma_start(out=ws[:], in_=w_scale.rearrange("o (p t) u -> p (o t u)", t=PACK))
+        load_w(0)
+        load_x(0)
+        nc.scalar.dma_start(out=rows[0:1, 0 : K * N], in_=g.rearrange("k n -> (k n)").unsqueeze(0))
+        nc.scalar.dma_start(out=rows[0:1, K * N : K * N + F], in_=bias.unsqueeze(0))
+        load_x(1)
+        nc.sync.dma_start(out=ed[:], in_=edge.rearrange("(c p) j -> p c j", p=P))
+        load_w(1)
+        load_x(2)
+        nc.sync.dma_start(out=es[0][:], in_=e1.rearrange("(c p) r -> p c r", p=P))
+        nc.sync.dma_start(out=es[1][:], in_=e2.rearrange("(c p) r -> p c r", p=P))
+        load_w(2)
+        load_x(3)
+
+        id_f = const.tile([P, P], F32, name="id_f")
+        id_b = const.tile([P, P], BF16, name="id_b")
+        make_identity(nc, id_f[:])
+        make_identity(nc, id_b[:])
+        nc.scalar.activation(out=dummy[:], in_=dummy[:], func=ACT.Exp)
+
+        gb = const.tile([P, 4 * 512], BF16, name="gb")
+
+        gb_bank = {}
+
+        def g_mm(h):
+            gb_bank[h] = ps_t.tile([P, 1024], BF16, name="t_bank")
+            for i in range(2):
+                nc.tensor.matmul(gb_bank[h][:, 512 * i : 512 * (i + 1)], lhsT=ones[:], rhs=rows[:, 1024 * h + 512 * i : 1024 * h + 512 * (i + 1)], start=True, stop=True)
+
+        def g_copy(k):
+            src = gb_bank[k // 2][:, 512 * (k % 2) : 512 * (k % 2 + 1)]
+            dst = gb[:, 512 * k : 512 * (k + 1)]
+            if k < K:
+                nc.scalar.copy(out=dst.rearrange("a (u p e) -> a u p e", u=2, e=2), in_=src.rearrange("a (p u e) -> a u p e", u=2, e=2))
+            else:
+                nc.scalar.copy(out=dst, in_=src)
+
+        def copy(eng, out, in_):
+            if eng == "A":
+                nc.scalar.copy(out=out, in_=in_)
+            else:
+                nc.vector.tensor_copy(out=out, in_=in_)
+
+        def quantised(name, width):
+            c = const.tile([P, width], U32, name=name + "_c", align_bytes=256)
+            s = const.tile([P, width], U8, name=name + "_s", align_bytes=256)
+            return c, s
+
+        def quantise(dst, src, lo=0, hi=512):
+            c, s = dst
+            nc.vector.quantize_mx(out=c[:, lo:hi].bitcast(FP8X4), scales=s[:, lo:hi], in_=src[:, 4 * lo : 4 * hi])
+
+        def turn(src, grouped, half, eng, sorted_words=False):
+            b = ps_t.tile([P, 2, 2, P], F32, name="t_bank")
+            for s in range(2):
+                words = src[:, 2 * half + s, :].bitcast(F32)
+                for u in range(2):
+                    nc.tensor.transpose(b[:, s, u, :], words[:, P * u : P * (u + 1)] if sorted_words else words[:, u : 256 : 2], id_f[:])
+            copy(eng, grouped[:].bitcast(F32)[:, 512 * half : 512 * (half + 1)].rearrange("p (s m u) -> p s m u", s=2, u=2), b[:].rearrange("p s u m -> p s m u"))
+
+        wq = [quantised(f"w{k}", F) for k in range(K)]
+        wide = {}
+        wgrp = {}
+
+        def widen(k, t, eng):
+            if k not in wide:
+                wide[k] = work.tile([P, PACK, F], BF16, name="wide")
+            src = wb[k][:, t, :].bitcast(FP8)
+            if eng == "A":
+                nc.scalar.activation(out=wide[k][:, t, :], in_=src, func=ACT.Copy, scale=ws[:, t : t + 1])
+            else:
+                nc.vector.tensor_scalar(out=wide[k][:, t, :], in0=src, scalar1=ws[:, t : t + 1], scalar2=None, op0=ALU.mult)
+
+        def w_inter(k):
+            wgrp[k] = work.tile([P, 4 * F], BF16, name="wgrp", align_bytes=64)
+            nc.vector.tensor_copy(out=wgrp[k][:].rearrange("p (c i t) -> p c t i", i=4, t=4), in_=wide[k][:].rearrange("p t (c i) -> p c t i", i=4))
+
+        def w_quant(k):
+            quantise(wq[k], wgrp[k])
+
+        xq = [quantised(f"xq{t}", N) for t in range(T)]
+        xgrp = {}
+
+        def x_turn(t, half, eng):
+            if t not in xgrp:
+                xgrp[t] = work.tile([P, 4 * N], BF16, name="xgrp", align_bytes=64)
+            turn(xs[t], xgrp[t], half, eng)
+
+        def x_quant(t):
+            quantise(xq[t], xgrp[t])
+
+        hq = {}
+        hgrp = {}
+
+        def h_unit(k, t, c, eng):
+            if (k, t) not in hgrp:
+                hgrp[k, t] = work.tile([P, 4 * F], BF16, name="hgrp", align_bytes=64, bufs=4)
+                hq[k, t] = quantised(f"h{k}{t}", F)
+            b = ps_h.tile([P, PACK, P], F32, name="h_bank")
+            f = slice(P * c, P * (c + 1))
+            for s in range(PACK):
+                m = slice(P * s, P * (s + 1))
+                nc.tensor.matmul_mx(out=b[:, s, :], lhsT=xq[t][0][:, m].bitcast(FP8X4), lhsT_scale=xq[t][1][:, m],
+                                    rhs=wq[k][0][:, f].bitcast(FP8X4), rhs_scale=wq[k][1][:, f], start=True, stop=True)
+            copy(eng, hgrp[k, t][:, 512 * c : 512 * (c + 1)].rearrange("p (n s) -> p n s", s=PACK), b[:].rearrange("p s n -> p n s"))
+
+        def h_quant(k, t, lo=0, hi=512):
+            quantise(hq[k, t], hgrp[k, t], lo, hi)
+
+        qq = [quantised(f"q{k}", N) for k in range(K)]
+        nmax = [const.tile([P, C], F32, name=f"nmax{k}") for k in range(K)]
+        sums = [const.tile([P, C], F32, name=f"sums{k}") for k in range(K)]
+        rec = [const.tile([P, C], F32, name=f"rec{k}") for k in range(K)]
+        ex = {}
+        qb = {}
+        qgrp = {}
+
+        mt = {}
+
+        def max0(stage):
+            if stage == 0:
+                mt["a"] = work.tile([P, C, 256], BF16, name="ma", bufs=1)
+                nc.vector.tensor_max(out=mt["a"][:], in0=ed[:, :, 0:256], in1=ed[:, :, 256:512])
+            elif stage == 1:
+                mt["b"] = work.tile([P, C, 128], BF16, name="mb", bufs=1)
+                nc.vector.tensor_max(out=mt["b"][:], in0=mt["a"][:, :, 0:128], in1=mt["a"][:, :, 128:256])
+            else:
+                nc.vector.tensor_reduce(out=nmax[0][:], in_=mt["b"][:], axis=AX.X, op=ALU.max, negate=True)
+
+        def max1(stage):
+            if stage == 0:
+                mt["c"] = work.tile([P, 2, N], BF16, name="mc", bufs=1)
+                nc.vector.tensor_max(out=mt["c"][:], in0=ed[:, 0:2, :], in1=ed[:, 2:4, :])
+            elif stage == 1:
+                mt["d"] = work.tile([P, N], BF16, name="md", bufs=1)
+                nc.vector.tensor_max(out=mt["d"][:], in0=mt["c"][:, 0, :], in1=mt["c"][:, 1, :])
+            elif stage == 2:
+                mt["e"] = ps_t.tile([P, C, P], BF16, name="t_bank")
+                for c in range(C):
+                    nc.tensor.transpose(mt["e"][:, c, :], mt["d"][:, P * c : P * (c + 1)], id_b[:])
+            else:
+                nc.vector.tensor_reduce(out=nmax[1][:], in_=mt["e"][:], axis=AX.X, op=ALU.max, negate=True)
+
+        def exp_row(k, r, src):
+            if k not in ex:
+                ex[k] = work.tile([P, C, N], F32, name="ex", bufs=3)
+            nc.scalar.activation(out=ex[k][:, r, :].rearrange("a (u p e) -> a u p e", u=2, e=2), in_=src.rearrange("a (p u e) -> a u p e", u=2, e=2), func=ACT.Exp, bias=nmax[k][:, r : r + 1], accum_out=sums[k][:, r : r + 1])
+
+        def exp0(r):
+            exp_row(0, r, ed[:, r, :])
+
+        ebank = {}
+
+        def p1_turn(half):
+            ebank[half] = ps_t.tile([P, 2, N], BF16, name="t_bank")
+            for i in range(2):
+                r = 2 * half + i
+                for c in range(C):
+                    nc.tensor.transpose(ebank[half][:, i, P * c : P * (c + 1)], ed[:, c, P * r : P * (r + 1)], id_b[:])
+
+        def exp1(r):
+            exp_row(1, r, ebank[r // 2][:, r % 2, :])
+
+        eq = [quantised(f"eq{i}", N) for i in range(2)]
+        egrp = {}
+
+        def e_turn(i, half, eng):
+            if i not in egrp:
+                egrp[i] = work.tile([P, 4 * N], BF16, name="egrp", align_bytes=64)
+            turn(es[i], egrp[i], half, eng)
+
+        def e_quant(i):
+            quantise(eq[i], egrp[i])
+
+        lg = const.tile([P, C, N], F32, name="lg")
+        pmax = const.tile([P, C], F32, name="pmax")
+
+        def logits(r):
+            b = ps_t.tile([P, N], F32, name="t_bank")
+            m = slice(P * r, P * (r + 1))
+            nc.tensor.matmul_mx(out=b[:], lhsT=eq[0][0][:, m].bitcast(FP8X4), lhsT_scale=eq[0][1][:, m],
+                                rhs=eq[1][0][:].bitcast(FP8X4), rhs_scale=eq[1][1][:], start=True, stop=True)
+            nc.vector.tensor_scalar(out=lg[:, r, :], in0=b[:], scalar1=0.0, scalar2=0.0, op0=ALU.max, op1=ALU.max, accum_out=pmax[:, r : r + 1])
+
+        def negate2():
+            nc.scalar.mul(out=nmax[2][:], in_=pmax[:], mul=-1.0)
+
+        def exp2(r):
+            exp_row(2, r, lg[:, r, :])
+
+        def recip(k):
+            nc.vector.reciprocal(out=rec[k][:], in_=sums[k][:])
+
+        def scale_q(k, r):
+            if k not in qb:
+                qb[k] = work.tile([P, C, N], BF16, name="qb")
+            nc.vector.scalar_tensor_tensor(out=qb[k][:, r, :], in0=ex[k][:, r, :], scalar=rec[k][:, r : r + 1], in1=gb[:, N * k : N * (k + 1)], op0=ALU.mult, op1=ALU.mult)
+
+        def q_turn(k, half, eng):
+            if k not in qgrp:
+                qgrp[k] = work.tile([P, 4 * N], BF16, name="qgrp", align_bytes=64)
+            turn(qb[k], qgrp[k], half, eng, sorted_words=True)
+
+        def q_quant(k):
+            quantise(qq[k], qgrp[k])
+
+        zb = {}
+
+        def z_mm(t, r, ks):
+            if (t, r) not in zb:
+                zb[t, r] = ps_z.tile([P, F], F32, name="z_bank")
+            m = slice(P * r, P * (r + 1))
+            for k in ks:
+                nc.tensor.matmul_mx(out=zb[t, r][:], lhsT=qq[k][0][:, m].bitcast(FP8X4), lhsT_scale=qq[k][1][:, m],
+                                    rhs=hq[k, t][0][:].bitcast(FP8X4), rhs_scale=hq[k, t][1][:], start=k == 0, stop=k == K - 1)
+
+        zo = {}
+
+        def z_add(t, r):
+            zo[t, r] = work.tile([P, F], F32, name="z_sum", bufs=4)
+            nc.vector.tensor_tensor(out=zo[t, r][:], in0=zb[t, r][:], in1=gb[:, K * N : K * N + F], op=ALU.add)
+
+        def z_out(t, r, eng):
+            o = work.tile([P, F], F32, name="z_out", bufs=6)
+            if eng == "A":
+                nc.scalar.activation(out=o[:], in_=zo[t, r][:], func=ACT.Relu)
+            else:
+                nc.vector.tensor_scalar_max(out=o[:], in0=zo[t, r][:], scalar1=0.0)
+            nc.sync.dma_start(out=out[t, P * r : P * (r + 1), :], in_=o[:])
+
+        widen(0, 2, "A")
+        widen(0, 1, "V")
+        widen(0, 3, "V")
+        g_mm(0)
+        g_copy(0)
+        g_copy(1)
+        widen(0, 0, "V")
+        x_turn(0, 0, "A")
+        x_turn(0, 1, "A")
+        w_inter(0)
+        w_quant(0)
+        x_quant(0)
+        x_turn(1, 0, "A")
+        x_turn(1, 1, "A")
+        h_unit(0, 0, 0, "A")
+        max1(0)
+        widen(1, 0, "V")
+        h_unit(0, 0, 3, "A")
+        h_unit(0, 0, 2, "A")
+        x_turn(2, 0, "A")
+        x_turn(2, 1, "A")
+        widen(1, 3, "V")
+        max1(1)
+        widen(1, 2, "V")
+        x_quant(1)
+        max0(0)
+        h_unit(0, 1, 0, "A")
+        widen(1, 1, "V")
+        h_unit(0, 1, 2, "A")
+        max0(1)
+        w_inter(1)
+        e_turn(0, 0, "A")
+        max1(2)
+        x_quant(2)
+        h_unit(0, 0, 1, "A")
+        h_unit(0, 1, 1, "A")
+        w_quant(1)
+        widen(2, 3, "V")
+        max1(3)
+        widen(2, 0, "V")
+        e_turn(0, 1, "A")
+        h_unit(0, 1, 3, "A")
+        h_unit(1, 2, 3, "A")
+        widen(2, 1, "V")
+        widen(2, 2, "V")
+        max0(2)
+        e_turn(1, 0, "A")
+        e_turn(1, 1, "A")
+        h_unit(0, 2, 2, "A")
+        p1_turn(0)
+        exp1(0)
+        h_unit(0, 2, 0, "A")
+        h_unit(0, 2, 3, "A")
+        h_quant(0, 0)
+        w_inter(2)
+        e_quant(0)
+        e_quant(1)
+        h_quant(0, 1)
+        h_unit(1, 2, 1, "V")
+        exp1(1)
+        exp0(0)
+        h_unit(0, 2, 1, "A")
+        logits(0)
+        exp0(2)
+        logits(2)
+        h_unit(1, 2, 0, "V")
+        exp0(3)
+        logits(1)
+        h_quant(0, 2)
+        p1_turn(1)
+        exp0(1)
+        exp1(2)
+        exp1(3)
+        recip(0)
+        h_unit(1, 1, 2, "A")
+        h_unit(1, 2, 2, "A")
+        w_quant(2)
+        logits(3)
+        scale_q(0, 0)
+        scale_q(0, 1)
+        recip(1)
+        scale_q(0, 2)
+        negate2()
+        scale_q(0, 3)
+        h_unit(2, 2, 2, "A")
+        scale_q(1, 0)
+        h_unit(2, 2, 0, "A")
+        scale_q(1, 2)
+        scale_q(1, 3)
+        h_unit(1, 1, 1, "A")
+        h_quant(1, 2)
+        q_turn(0, 0, "A")
+        h_unit(1, 1, 3, "A")
+        x_turn(3, 1, "A")
+        h_unit(1, 1, 0, "A")
+        h_unit(1, 0, 3, "V")
+        q_turn(1, 1, "A")
+        q_turn(0, 1, "A")
+        scale_q(1, 1)
+        h_unit(1, 0, 2, "V")
+        exp2(2)
+        h_unit(2, 1, 2, "V")
+        q_turn(1, 0, "V")
+        exp2(0)
+        g_mm(1)
+        exp2(3)
+        exp2(1)
+        h_unit(2, 2, 1, "V")
+        q_quant(0)
+        q_quant(1)
+        recip(2)
+        h_unit(2, 1, 0, "A")
+        x_turn(3, 0, "A")
+        g_copy(2)
+        h_quant(1, 1)
+        h_unit(1, 0, 1, "A")
+        h_unit(2, 1, 1, "A")
+        z_mm(2, 1, (0, 1))
+        scale_q(2, 0)
+        scale_q(2, 3)
+        z_mm(2, 3, (0, 1))
+        h_unit(2, 2, 3, "A")
+        scale_q(2, 2)
+        scale_q(2, 1)
+        g_copy(3)
+        z_mm(2, 2, (0, 1))
+        h_quant(2, 2)
+        h_unit(2, 0, 3, "A")
+        h_unit(2, 1, 3, "A")
+        q_turn(2, 1, "A")
+        q_turn(2, 0, "V")
+        h_unit(2, 0, 1, "A")
+        q_quant(2)
+        x_quant(3)
+        z_mm(1, 0, (0, 1))
+        h_unit(2, 0, 2, "A")
+        h_quant(2, 1)
+        h_unit(2, 0, 0, "A")
+        z_mm(2, 2, (2,))
+        z_mm(2, 1, (2,))
+        h_unit(1, 0, 0, "A")
+        z_mm(2, 3, (2,))
+        h_unit(2, 3, 0, "A")
+        z_add(2, 1)
+        z_mm(1, 0, (2,))
+        z_mm(1, 2, (0, 1))
+        h_quant(1, 0)
+        z_add(2, 3)
+        h_unit(0, 3, 1, "A")
+        h_quant(2, 0)
+        h_unit(1, 3, 3, "A")
+        z_add(2, 2)
+        z_mm(1, 2, (2,))
+        z_mm(0, 0, (0, 1))
+        z_out(2, 3, "A")
+        h_unit(2, 3, 2, "A")
+        h_unit(0, 3, 2, "A")
+        z_mm(2, 0, (0, 1))
+        z_mm(0, 0, (2,))
+        h_unit(1, 3, 2, "A")
+        z_add(1, 0)
+        z_out(2, 1, "V")
+        z_mm(2, 0, (2,))
+        h_unit(1, 3, 0, "A")
+        z_mm(0, 3, (0, 1))
+        h_unit(0, 3, 0, "A")
+        z_out(2, 2, "V")
+        z_add(0, 0)
+        z_add(1, 2)
+        z_mm(0, 3, (2,))
+        z_out(0, 0, "V")
+        z_out(1, 2, "A")
+        z_out(1, 0, "V")
+        h_unit(0, 3, 3, "A")
+        z_add(2, 0)
+        z_add(0, 3)
+        z_mm(1, 3, (0, 1))
+        h_unit(2, 3, 3, "A")
+        z_out(0, 3, "V")
+        z_mm(0, 2, (0, 1))
+        z_out(2, 0, "V")
+        z_mm(0, 2, (2,))
+        z_mm(1, 3, (2,))
+        h_quant(0, 3)
+        h_unit(1, 3, 1, "A")
+        z_add(0, 2)
+        z_add(1, 3)
+        h_quant(1, 3)
+        h_unit(2, 3, 1, "A")
+        z_mm(0, 1, (0, 1))
+        h_quant(2, 3)
+        z_mm(1, 1, (0, 1))
+        z_mm(1, 1, (2,))
+        z_out(0, 2, "A")
+        z_add(1, 1)
+        z_mm(0, 1, (2,))
+        z_mm(3, 3, (0, 1))
+        z_mm(3, 3, (2,))
+        z_out(1, 3, "A")
+        z_mm(3, 2, (0, 1))
+        z_add(0, 1)
+        z_mm(3, 2, (2,))
+        z_mm(3, 0, (0, 1))
+        z_out(1, 1, "A")
+        z_mm(3, 0, (2,))
+        z_add(3, 3)
+        z_out(0, 1, "A")
+        z_out(3, 3, "A")
+        z_add(3, 2)
+        z_mm(3, 1, (0, 1))
+        z_mm(3, 1, (2,))
+        z_add(3, 0)
+        z_add(3, 1)
+        z_out(3, 2, "A")
+        z_out(3, 0, "A")
+        z_out(3, 1, "V")

@@ -31,7 +31,7 @@ def tile_graphwavenetdiffusionconv_kernel(tc, x, edge, e1, e2, w_bytes, w_scale,
         ps_z = ctx.enter_context(tc.psum_pool(name="ps_z", bufs=4))
         ctx.enter_context(tc.manual_schedule())
 
-        rows = const.tile([P, 4 * 512], BF16, name="rows")
+        rows = const.tile([P, K * N], BF16, name="rows")
         ones = const.tile([P, P], BF16, name="ones")
         dummy = const.tile([P, 1], F32, name="dummy")
         nc.vector.memset(rows[:].bitcast(U32), 0)
@@ -43,25 +43,28 @@ def tile_graphwavenetdiffusionconv_kernel(tc, x, edge, e1, e2, w_bytes, w_scale,
         ed = const.tile([P, C, N], BF16, name="ed")
         es = [const.tile([P, C, R], BF16, name=f"e{i}") for i in range(2)]
 
-        def load_w(k):
-            nc.sync.dma_start(out=wb[k][:], in_=w_bytes[k].rearrange("(p t) f -> p t f", t=PACK))
+        def load_w(k, lo=0, hi=PACK):
+            nc.sync.dma_start(out=wb[k][:, lo:hi, :], in_=w_bytes[k].rearrange("(p t) f -> p t f", t=PACK)[:, lo:hi, :])
 
-        def load_x(t):
-            nc.sync.dma_start(out=xs[t][:], in_=x[t].rearrange("(m s) d -> m s d", s=PACK))
+        def load_x(t, lo=0, hi=PACK):
+            nc.sync.dma_start(out=xs[t][:, lo:hi, :], in_=x[t].rearrange("(m s) d -> m s d", s=PACK)[:, lo:hi, :])
 
-        nc.sync.dma_start(out=ws[:], in_=w_scale.rearrange("o (p t) u -> p (o t u)", t=PACK))
-        load_w(0)
-        load_x(0)
-        nc.scalar.dma_start(out=rows[0:1, 0 : K * N], in_=g.rearrange("k n -> (k n)").unsqueeze(0))
-        nc.scalar.dma_start(out=rows[0:1, K * N : K * N + F], in_=bias.unsqueeze(0))
-        load_x(1)
-        nc.sync.dma_start(out=ed[:], in_=edge.rearrange("(c p) j -> p c j", p=P))
+        nc.scalar.dma_start(out=ws[:], in_=w_scale.rearrange("o (p t) u -> p (o t u)", t=PACK))
+        load_w(0, 0, 2)
+        nc.sync.dma_start(out=rows[0:1, 0 : K * N], in_=g.rearrange("k n -> (k n)").unsqueeze(0))
+        load_w(0, 2, 4)
         load_w(1)
-        load_x(2)
-        nc.sync.dma_start(out=es[0][:], in_=e1.rearrange("(c p) r -> p c r", p=P))
-        nc.sync.dma_start(out=es[1][:], in_=e2.rearrange("(c p) r -> p c r", p=P))
+        load_x(0, 2, 4)
+        load_x(0, 0, 2)
+        load_x(1)
         load_w(2)
+        nc.sync.dma_start(out=es[0][:], in_=e1.rearrange("(c p) r -> p c r", p=P))
+        nc.sync.dma_start(out=ed[:], in_=edge.rearrange("(c p) j -> p c j", p=P))
+        nc.sync.dma_start(out=es[1][:], in_=e2.rearrange("(c p) r -> p c r", p=P))
         load_x(3)
+        load_x(2)
+        bias_bc = const.tile([P, F], BF16, name="bias_bc")
+        nc.sync.dma_start(out=bias_bc[:], in_=bias.partition_broadcast(P))
 
         id_f = const.tile([P, P], F32, name="id_f")
         id_b = const.tile([P, P], BF16, name="id_b")
@@ -69,22 +72,20 @@ def tile_graphwavenetdiffusionconv_kernel(tc, x, edge, e1, e2, w_bytes, w_scale,
         make_identity(nc, id_b[:])
         nc.scalar.activation(out=dummy[:], in_=dummy[:], func=ACT.Exp)
 
-        gb = const.tile([P, 4 * 512], BF16, name="gb")
+        gb = const.tile([P, K * N], BF16, name="gb")
 
         gb_bank = {}
 
-        def g_mm(h):
-            gb_bank[h] = ps_t.tile([P, 1024], BF16, name="t_bank")
-            for i in range(2):
-                nc.tensor.matmul(gb_bank[h][:, 512 * i : 512 * (i + 1)], lhsT=ones[:], rhs=rows[:, 1024 * h + 512 * i : 1024 * h + 512 * (i + 1)], start=True, stop=True)
+        def g_mm():
+            for h in range(2):
+                gb_bank[h] = ps_t.tile([P, 1024], BF16, name="t_bank")
+            for k in range(K):
+                nc.tensor.matmul(gb_bank[k // 2][:, N * (k % 2) : N * (k % 2 + 1)], lhsT=ones[:], rhs=rows[:, N * k : N * (k + 1)], start=True, stop=True)
 
-        def g_copy(k):
-            src = gb_bank[k // 2][:, 512 * (k % 2) : 512 * (k % 2 + 1)]
-            dst = gb[:, 512 * k : 512 * (k + 1)]
-            if k < K:
-                nc.scalar.copy(out=dst.rearrange("a (u p e) -> a u p e", u=2, e=2), in_=src.rearrange("a (p u e) -> a u p e", u=2, e=2))
-            else:
-                nc.scalar.copy(out=dst, in_=src)
+        def g_copy(h):
+            for k in ((0, 1), (2,))[h]:
+                nc.scalar.copy(out=gb[:, N * k : N * (k + 1)].rearrange("a (u p e) -> a u p e", u=2, e=2),
+                               in_=gb_bank[h][:, N * (k % 2) : N * (k % 2 + 1)].rearrange("a (p u e) -> a u p e", u=2, e=2))
 
         def copy(eng, out, in_):
             if eng == "A":
@@ -256,242 +257,242 @@ def tile_graphwavenetdiffusionconv_kernel(tc, x, edge, e1, e2, w_bytes, w_scale,
             quantise(qq[k], qgrp[k])
 
         zb = {}
-
-        def z_mm(t, r, ks):
-            if (t, r) not in zb:
-                zb[t, r] = ps_z.tile([P, F], F32, name="z_bank")
-            m = slice(P * r, P * (r + 1))
-            for k in ks:
-                nc.tensor.matmul_mx(out=zb[t, r][:], lhsT=qq[k][0][:, m].bitcast(FP8X4), lhsT_scale=qq[k][1][:, m],
-                                    rhs=hq[k, t][0][:].bitcast(FP8X4), rhs_scale=hq[k, t][1][:], start=k == 0, stop=k == K - 1)
-
         zo = {}
 
-        def z_add(t, r):
-            zo[t, r] = work.tile([P, F], F32, name="z_sum", bufs=4)
-            nc.vector.tensor_tensor(out=zo[t, r][:], in0=zb[t, r][:], in1=gb[:, K * N : K * N + F], op=ALU.add)
+        def z_mm(t, r, ks, lo=0, hi=F):
+            if (t, r, lo) not in zb:
+                zb[t, r, lo] = ps_z.tile([P, hi - lo], F32, name="z_bank")
+            m = slice(P * r, P * (r + 1))
+            for k in ks:
+                nc.tensor.matmul_mx(out=zb[t, r, lo][:], lhsT=qq[k][0][:, m].bitcast(FP8X4), lhsT_scale=qq[k][1][:, m],
+                                    rhs=hq[k, t][0][:, lo:hi].bitcast(FP8X4), rhs_scale=hq[k, t][1][:, lo:hi], start=k == 0, stop=k == K - 1)
 
-        def z_out(t, r, eng):
-            o = work.tile([P, F], F32, name="z_out", bufs=6)
+        def z_add(t, r, lo=0, hi=F):
+            zo[t, r, lo] = work.tile([P, hi - lo], F32, name="z_sum", bufs=4)
+            nc.vector.tensor_tensor(out=zo[t, r, lo][:], in0=zb[t, r, lo][:], in1=bias_bc[:, lo:hi], op=ALU.add)
+
+        def z_out(t, r, eng, lo=0, hi=F):
+            o = work.tile([P, hi - lo], F32, name="z_out", bufs=6)
             if eng == "A":
-                nc.scalar.activation(out=o[:], in_=zo[t, r][:], func=ACT.Relu)
+                nc.scalar.activation(out=o[:], in_=zo[t, r, lo][:], func=ACT.Relu)
             else:
-                nc.vector.tensor_scalar_max(out=o[:], in0=zo[t, r][:], scalar1=0.0)
-            nc.sync.dma_start(out=out[t, P * r : P * (r + 1), :], in_=o[:])
+                nc.vector.tensor_scalar_max(out=o[:], in0=zo[t, r, lo][:], scalar1=0.0)
+            nc.sync.dma_start(out=out[t, P * r : P * (r + 1), lo:hi], in_=o[:])
 
-        widen(0, 2, "A")
-        widen(0, 1, "V")
-        widen(0, 3, "V")
-        g_mm(0)
-        g_copy(0)
-        g_copy(1)
+        widen(0, 3, "A")
+        g_mm()
         widen(0, 0, "V")
-        x_turn(0, 0, "A")
-        x_turn(0, 1, "A")
+        widen(0, 1, "V")
+        g_copy(0)
+        widen(0, 2, "V")
+        widen(1, 2, "V")
         w_inter(0)
+        g_copy(1)
+        widen(1, 3, "V")
+        widen(1, 0, "A")
         w_quant(0)
-        x_quant(0)
+        x_turn(0, 1, "A")
+        x_turn(0, 0, "A")
+        widen(1, 1, "A")
         x_turn(1, 0, "A")
         x_turn(1, 1, "A")
-        h_unit(0, 0, 0, "A")
-        max1(0)
-        widen(1, 0, "V")
-        h_unit(0, 0, 3, "A")
-        h_unit(0, 0, 2, "A")
-        x_turn(2, 0, "A")
-        x_turn(2, 1, "A")
-        widen(1, 3, "V")
-        max1(1)
-        widen(1, 2, "V")
+        x_quant(0)
+        w_inter(1)
+        widen(2, 1, "V")
+        widen(2, 2, "A")
         x_quant(1)
         max0(0)
-        h_unit(0, 1, 0, "A")
-        widen(1, 1, "V")
-        h_unit(0, 1, 2, "A")
-        max0(1)
-        w_inter(1)
-        e_turn(0, 0, "A")
-        max1(2)
-        x_quant(2)
-        h_unit(0, 0, 1, "A")
-        h_unit(0, 1, 1, "A")
-        w_quant(1)
-        widen(2, 3, "V")
-        max1(3)
+        max1(0)
         widen(2, 0, "V")
-        e_turn(0, 1, "A")
-        h_unit(0, 1, 3, "A")
-        h_unit(1, 2, 3, "A")
-        widen(2, 1, "V")
-        widen(2, 2, "V")
-        max0(2)
-        e_turn(1, 0, "A")
+        h_unit(0, 0, 0, "A")
+        max0(1)
+        h_unit(0, 0, 1, "A")
+        e_turn(0, 0, "A")
+        h_unit(0, 0, 2, "A")
+        max1(1)
+        h_unit(0, 0, 3, "A")
         e_turn(1, 1, "A")
-        h_unit(0, 2, 2, "A")
-        p1_turn(0)
-        exp1(0)
-        h_unit(0, 2, 0, "A")
-        h_unit(0, 2, 3, "A")
-        h_quant(0, 0)
-        w_inter(2)
-        e_quant(0)
-        e_quant(1)
-        h_quant(0, 1)
-        h_unit(1, 2, 1, "V")
-        exp1(1)
-        exp0(0)
-        h_unit(0, 2, 1, "A")
-        logits(0)
+        e_turn(1, 0, "A")
+        w_quant(1)
+        h_unit(0, 1, 0, "A")
+        widen(2, 3, "V")
+        max0(2)
+        h_unit(0, 1, 1, "V")
         exp0(2)
-        logits(2)
-        h_unit(1, 2, 0, "V")
-        exp0(3)
-        logits(1)
-        h_quant(0, 2)
-        p1_turn(1)
         exp0(1)
-        exp1(2)
+        e_turn(0, 1, "V")
+        max1(2)
+        h_unit(0, 1, 2, "A")
+        exp0(0)
+        max1(3)
+        h_unit(0, 1, 3, "V")
+        e_quant(0)
+        p1_turn(0)
+        e_quant(1)
+        exp1(1)
+        h_unit(1, 0, 0, "V")
+        exp1(0)
+        p1_turn(1)
         exp1(3)
-        recip(0)
-        h_unit(1, 1, 2, "A")
-        h_unit(1, 2, 2, "A")
-        w_quant(2)
+        exp1(2)
+        h_unit(1, 0, 1, "V")
+        h_unit(1, 0, 2, "A")
+        w_inter(2)
+        logits(2)
+        h_unit(1, 0, 3, "A")
         logits(3)
-        scale_q(0, 0)
-        scale_q(0, 1)
-        recip(1)
-        scale_q(0, 2)
-        negate2()
-        scale_q(0, 3)
-        h_unit(2, 2, 2, "A")
-        scale_q(1, 0)
-        h_unit(2, 2, 0, "A")
-        scale_q(1, 2)
-        scale_q(1, 3)
-        h_unit(1, 1, 1, "A")
-        h_quant(1, 2)
-        q_turn(0, 0, "A")
-        h_unit(1, 1, 3, "A")
-        x_turn(3, 1, "A")
+        exp0(3)
         h_unit(1, 1, 0, "A")
-        h_unit(1, 0, 3, "V")
-        q_turn(1, 1, "A")
-        q_turn(0, 1, "A")
-        scale_q(1, 1)
-        h_unit(1, 0, 2, "V")
-        exp2(2)
-        h_unit(2, 1, 2, "V")
-        q_turn(1, 0, "V")
-        exp2(0)
-        g_mm(1)
-        exp2(3)
-        exp2(1)
-        h_unit(2, 2, 1, "V")
-        q_quant(0)
-        q_quant(1)
-        recip(2)
-        h_unit(2, 1, 0, "A")
+        h_unit(1, 1, 1, "A")
+        recip(1)
+        x_turn(2, 1, "A")
+        h_unit(1, 1, 2, "A")
         x_turn(3, 0, "A")
-        g_copy(2)
-        h_quant(1, 1)
-        h_unit(1, 0, 1, "A")
-        h_unit(2, 1, 1, "A")
-        z_mm(2, 1, (0, 1))
-        scale_q(2, 0)
-        scale_q(2, 3)
-        z_mm(2, 3, (0, 1))
-        h_unit(2, 2, 3, "A")
-        scale_q(2, 2)
-        scale_q(2, 1)
-        g_copy(3)
-        z_mm(2, 2, (0, 1))
-        h_quant(2, 2)
-        h_unit(2, 0, 3, "A")
-        h_unit(2, 1, 3, "A")
-        q_turn(2, 1, "A")
-        q_turn(2, 0, "V")
-        h_unit(2, 0, 1, "A")
-        q_quant(2)
-        x_quant(3)
-        z_mm(1, 0, (0, 1))
-        h_unit(2, 0, 2, "A")
-        h_quant(2, 1)
-        h_unit(2, 0, 0, "A")
-        z_mm(2, 2, (2,))
-        z_mm(2, 1, (2,))
-        h_unit(1, 0, 0, "A")
-        z_mm(2, 3, (2,))
-        h_unit(2, 3, 0, "A")
-        z_add(2, 1)
-        z_mm(1, 0, (2,))
-        z_mm(1, 2, (0, 1))
         h_quant(1, 0)
-        z_add(2, 3)
-        h_unit(0, 3, 1, "A")
-        h_quant(2, 0)
-        h_unit(1, 3, 3, "A")
-        z_add(2, 2)
-        z_mm(1, 2, (2,))
-        z_mm(0, 0, (0, 1))
-        z_out(2, 3, "A")
-        h_unit(2, 3, 2, "A")
-        h_unit(0, 3, 2, "A")
-        z_mm(2, 0, (0, 1))
-        z_mm(0, 0, (2,))
-        h_unit(1, 3, 2, "A")
-        z_add(1, 0)
-        z_out(2, 1, "V")
-        z_mm(2, 0, (2,))
-        h_unit(1, 3, 0, "A")
-        z_mm(0, 3, (0, 1))
-        h_unit(0, 3, 0, "A")
-        z_out(2, 2, "V")
-        z_add(0, 0)
-        z_add(1, 2)
-        z_mm(0, 3, (2,))
-        z_out(0, 0, "V")
-        z_out(1, 2, "A")
-        z_out(1, 0, "V")
-        h_unit(0, 3, 3, "A")
-        z_add(2, 0)
-        z_add(0, 3)
-        z_mm(1, 3, (0, 1))
-        h_unit(2, 3, 3, "A")
-        z_out(0, 3, "V")
+        h_unit(1, 1, 3, "A")
+        recip(0)
+        w_quant(2)
+        h_quant(0, 0)
+        scale_q(0, 1)
+        scale_q(1, 3)
+        logits(0)
+        h_quant(0, 1)
+        scale_q(0, 0)
+        scale_q(1, 2)
+        h_unit(2, 0, 0, "A")
+        x_turn(2, 0, "A")
+        h_unit(2, 0, 1, "A")
+        h_unit(2, 0, 2, "A")
+        x_turn(3, 1, "A")
+        logits(1)
+        h_unit(2, 0, 3, "A")
+        negate2()
+        scale_q(1, 1)
+        h_unit(2, 1, 0, "A")
+        q_turn(1, 1, "A")
+        scale_q(0, 2)
+        q_turn(0, 0, "A")
+        scale_q(0, 3)
+        h_unit(2, 1, 1, "A")
+        scale_q(1, 0)
+        x_quant(2)
+        h_unit(2, 1, 2, "V")
+        exp2(1)
+        exp2(3)
+        h_unit(2, 1, 3, "V")
+        q_turn(0, 1, "V")
+        exp2(2)
+        q_turn(1, 0, "A")
+        h_unit(2, 2, 0, "V")
+        q_quant(0)
+        h_unit(2, 2, 1, "A")
+        exp2(0)
+        q_quant(1)
+        h_unit(2, 2, 2, "A")
+        h_unit(2, 2, 3, "A")
+        recip(2)
         z_mm(0, 2, (0, 1))
-        z_out(2, 0, "V")
-        z_mm(0, 2, (2,))
-        z_mm(1, 3, (2,))
-        h_quant(0, 3)
-        h_unit(1, 3, 1, "A")
-        z_add(0, 2)
-        z_add(1, 3)
-        h_quant(1, 3)
-        h_unit(2, 3, 1, "A")
-        z_mm(0, 1, (0, 1))
-        h_quant(2, 3)
+        h_quant(1, 1)
+        h_unit(1, 2, 0, "A")
+        h_unit(1, 2, 1, "A")
+        scale_q(2, 1)
+        scale_q(2, 0)
+        z_mm(1, 3, (0, 1))
+        scale_q(2, 3)
+        h_unit(1, 2, 2, "A")
+        scale_q(2, 2)
+        h_unit(1, 2, 3, "A")
+        q_turn(2, 0, "A")
+        h_quant(2, 0)
+        q_turn(2, 1, "V")
+        q_quant(2)
+        h_unit(0, 2, 0, "A")
+        h_unit(0, 2, 1, "A")
         z_mm(1, 1, (0, 1))
+        z_mm(0, 3, (0, 1))
+        h_unit(0, 2, 2, "A")
+        z_mm(0, 2, (2,))
+        h_quant(2, 1)
+        x_quant(3)
+        h_unit(0, 2, 3, "A")
+        z_mm(1, 3, (2,))
+        z_add(0, 2)
         z_mm(1, 1, (2,))
-        z_out(0, 2, "A")
+        h_unit(0, 3, 0, "A")
+        z_mm(0, 3, (2,))
+        z_add(1, 3)
+        h_quant(2, 2)
         z_add(1, 1)
+        h_unit(0, 3, 1, "A")
+        h_quant(0, 2)
+        z_mm(0, 0, (0, 1))
+        h_unit(0, 3, 2, "A")
+        z_mm(0, 0, (2,))
+        h_unit(0, 3, 3, "A")
+        z_out(0, 2, "V")
+        z_out(1, 3, "V")
+        z_mm(0, 1, (0, 1))
+        h_unit(1, 3, 0, "A")
         z_mm(0, 1, (2,))
-        z_mm(3, 3, (0, 1))
-        z_mm(3, 3, (2,))
-        z_out(1, 3, "A")
-        z_mm(3, 2, (0, 1))
+        z_add(0, 0)
+        h_unit(1, 3, 1, "A")
+        z_mm(1, 0, (0, 1))
+        z_add(0, 3)
+        z_out(1, 1, "V")
+        z_out(0, 0, "A")
+        h_unit(1, 3, 2, "A")
+        z_mm(1, 0, (2,))
+        h_quant(1, 2)
+        h_unit(1, 3, 3, "A")
+        h_quant(0, 3)
+        z_mm(2, 0, (0, 1))
+        z_add(1, 0)
+        z_out(1, 0, "A")
+        z_mm(2, 0, (2,))
+        h_unit(2, 3, 0, "A")
+        z_mm(2, 3, (0, 1))
+        z_out(0, 3, "V")
         z_add(0, 1)
-        z_mm(3, 2, (2,))
+        h_unit(2, 3, 1, "A")
+        z_mm(2, 2, (0, 1))
+        z_add(2, 0)
+        z_out(0, 1, "V")
+        h_quant(1, 3)
+        z_mm(2, 2, (2,))
+        z_out(2, 0, "V")
+        z_add(2, 2)
+        h_unit(2, 3, 2, "A")
+        h_unit(2, 3, 3, "A")
+        z_mm(2, 3, (2,))
+        z_mm(2, 1, (0, 1))
+        z_mm(1, 2, (0, 1))
+        z_mm(2, 1, (2,))
+        z_add(2, 3)
+        z_out(2, 2, "A")
+        h_quant(2, 3)
+        z_mm(1, 2, (2,))
+        z_out(2, 3, "A")
         z_mm(3, 0, (0, 1))
-        z_out(1, 1, "A")
+        z_add(2, 1)
         z_mm(3, 0, (2,))
-        z_add(3, 3)
-        z_out(0, 1, "A")
-        z_out(3, 3, "A")
-        z_add(3, 2)
+        z_mm(3, 2, (0, 1))
+        z_mm(3, 2, (2,))
         z_mm(3, 1, (0, 1))
+        z_add(1, 2)
+        z_out(2, 1, "A")
         z_mm(3, 1, (2,))
+        z_mm(3, 3, (0, 1), 0, 256)
         z_add(3, 0)
+        z_out(1, 2, "V")
+        z_mm(3, 3, (2,), 0, 256)
+        z_add(3, 2)
         z_add(3, 1)
-        z_out(3, 2, "A")
+        z_add(3, 3, 0, 256)
         z_out(3, 0, "A")
+        z_out(3, 2, "A")
+        z_mm(3, 3, (0, 1), 256, 512)
         z_out(3, 1, "V")
+        z_mm(3, 3, (2,), 256, 512)
+        z_add(3, 3, 256, 512)
+        z_out(3, 3, "V", 0, 256)
+        z_out(3, 3, "V", 256, 512)

from contextlib import ExitStack

import concourse.mybir as mybir
from concourse.masks import make_identity

T, N, D, F, R, K = 4, 512, 512, 512, 512, 3
FLOPS = 2 * N * N * R + 2 * K * T * N * D * F + 2 * K * T * N * N * F

P = 128
PACK = 4
C = 4

F32 = mybir.dt.float32
BF16 = mybir.dt.bfloat16
U32 = mybir.dt.uint32
U8 = mybir.dt.uint8
FP8 = mybir.dt.float8_e4m3fn
FP8X4 = mybir.dt.float8_e4m3fn_x4
ALU = mybir.AluOpType
ACT = mybir.ActivationFunctionType
AX = mybir.AxisListType


def tile_graphwavenetdiffusionconv_kernel(tc, x, edge, e1, e2, w_bytes, w_scale, g, bias, out):
    nc = tc.nc
    with ExitStack() as ctx:
        const = ctx.enter_context(tc.tile_pool(name="const", bufs=1))
        work = ctx.enter_context(tc.tile_pool(name="work", bufs=2))
        ps_h = ctx.enter_context(tc.psum_pool(name="ps_h", bufs=2))
        ps_t = ctx.enter_context(tc.psum_pool(name="ps_t", bufs=2))
        ps_z = ctx.enter_context(tc.psum_pool(name="ps_z", bufs=4))
        ctx.enter_context(tc.manual_schedule())

        rows = const.tile([P, K * N], BF16, name="rows")
        ones = const.tile([P, P], BF16, name="ones")
        dummy = const.tile([P, 1], F32, name="dummy")
        nc.vector.memset(rows[:].bitcast(U32), 0)
        nc.vector.memset(ones[:], 1.0)
        nc.gpsimd.memset(dummy[:], 0.0)
        ws = const.tile([P, PACK], F32, name="ws")
        wb = [const.tile([P, PACK, F], U8, name=f"wb{k}") for k in range(K)]
        xs = [const.tile([P, PACK, D], BF16, name=f"x{t}") for t in range(T)]
        ed = const.tile([P, C, N], BF16, name="ed")
        es = [const.tile([P, C, R], BF16, name=f"e{i}") for i in range(2)]

        def load_w(k, lo=0, hi=PACK):
            nc.sync.dma_start(out=wb[k][:, lo:hi, :], in_=w_bytes[k].rearrange("(p t) f -> p t f", t=PACK)[:, lo:hi, :])

        def load_x(t, lo=0, hi=PACK):
            nc.sync.dma_start(out=xs[t][:, lo:hi, :], in_=x[t].rearrange("(m s) d -> m s d", s=PACK)[:, lo:hi, :])

        nc.scalar.dma_start(out=ws[:], in_=w_scale.rearrange("o (p t) u -> p (o t u)", t=PACK))
        load_w(0, 0, 2)
        nc.sync.dma_start(out=rows[0:1, 0 : K * N], in_=g.rearrange("k n -> (k n)").unsqueeze(0))
        load_w(0, 2, 4)
        load_w(1)
        load_x(0, 2, 4)
        load_x(0, 0, 2)
        load_x(1)
        load_w(2)
        nc.sync.dma_start(out=es[0][:], in_=e1.rearrange("(c p) r -> p c r", p=P))
        nc.sync.dma_start(out=ed[:], in_=edge.rearrange("(c p) j -> p c j", p=P))
        nc.sync.dma_start(out=es[1][:], in_=e2.rearrange("(c p) r -> p c r", p=P))
        load_x(3)
        load_x(2)
        bias_bc = const.tile([P, F], BF16, name="bias_bc")
        nc.sync.dma_start(out=bias_bc[:], in_=bias.partition_broadcast(P))

        id_f = const.tile([P, P], F32, name="id_f")
        id_b = const.tile([P, P], BF16, name="id_b")
        make_identity(nc, id_f[:])
        make_identity(nc, id_b[:])
        nc.scalar.activation(out=dummy[:], in_=dummy[:], func=ACT.Exp)

        gb = const.tile([P, K * N], BF16, name="gb")

        gb_bank = {}

        def g_mm():
            for h in range(2):
                gb_bank[h] = ps_t.tile([P, 1024], BF16, name="t_bank")
            for k in range(K):
                nc.tensor.matmul(gb_bank[k // 2][:, N * (k % 2) : N * (k % 2 + 1)], lhsT=ones[:], rhs=rows[:, N * k : N * (k + 1)], start=True, stop=True)

        def g_copy(h):
            for k in ((0, 1), (2,))[h]:
                nc.scalar.copy(out=gb[:, N * k : N * (k + 1)].rearrange("a (u p e) -> a u p e", u=2, e=2),
                               in_=gb_bank[h][:, N * (k % 2) : N * (k % 2 + 1)].rearrange("a (p u e) -> a u p e", u=2, e=2))

        def copy(eng, out, in_):
            if eng == "A":
                nc.scalar.copy(out=out, in_=in_)
            else:
                nc.vector.tensor_copy(out=out, in_=in_)

        def quantised(name, width):
            c = const.tile([P, width], U32, name=name + "_c", align_bytes=256)
            s = const.tile([P, width], U8, name=name + "_s", align_bytes=256)
            return c, s

        def quantise(dst, src, lo=0, hi=512):
            c, s = dst
            nc.vector.quantize_mx(out=c[:, lo:hi].bitcast(FP8X4), scales=s[:, lo:hi], in_=src[:, 4 * lo : 4 * hi])

        def turn(src, grouped, half, eng, sorted_words=False):
            b = ps_t.tile([P, 2, 2, P], F32, name="t_bank")
            for s in range(2):
                words = src[:, 2 * half + s, :].bitcast(F32)
                for u in range(2):
                    nc.tensor.transpose(b[:, s, u, :], words[:, P * u : P * (u + 1)] if sorted_words else words[:, u : 256 : 2], id_f[:])
            copy(eng, grouped[:].bitcast(F32)[:, 512 * half : 512 * (half + 1)].rearrange("p (s m u) -> p s m u", s=2, u=2), b[:].rearrange("p s u m -> p s m u"))

        wq = [quantised(f"w{k}", F) for k in range(K)]
        wide = {}
        wgrp = {}

        def widen(k, t, eng):
            if k not in wide:
                wide[k] = work.tile([P, PACK, F], BF16, name="wide")
            src = wb[k][:, t, :].bitcast(FP8)
            if eng == "A":
                nc.scalar.activation(out=wide[k][:, t, :], in_=src, func=ACT.Copy, scale=ws[:, t : t + 1])
            else:
                nc.vector.tensor_scalar(out=wide[k][:, t, :], in0=src, scalar1=ws[:, t : t + 1], scalar2=None, op0=ALU.mult)

        def w_inter(k):
            wgrp[k] = work.tile([P, 4 * F], BF16, name="wgrp", align_bytes=64)
            nc.vector.tensor_copy(out=wgrp[k][:].rearrange("p (c i t) -> p c t i", i=4, t=4), in_=wide[k][:].rearrange("p t (c i) -> p c t i", i=4))

        def w_quant(k):
            quantise(wq[k], wgrp[k])

        xq = [quantised(f"xq{t}", N) for t in range(T)]
        xgrp = {}

        def x_turn(t, half, eng):
            if t not in xgrp:
                xgrp[t] = work.tile([P, 4 * N], BF16, name="xgrp", align_bytes=64)
            turn(xs[t], xgrp[t], half, eng)

        def x_quant(t):
            quantise(xq[t], xgrp[t])

        hq = {}
        hgrp = {}

        def h_unit(k, t, c, eng):
            if (k, t) not in hgrp:
                hgrp[k, t] = work.tile([P, 4 * F], BF16, name="hgrp", align_bytes=64, bufs=4)
                hq[k, t] = quantised(f"h{k}{t}", F)
            b = ps_h.tile([P, PACK, P], F32, name="h_bank")
            f = slice(P * c, P * (c + 1))
            for s in range(PACK):
                m = slice(P * s, P * (s + 1))
                nc.tensor.matmul_mx(out=b[:, s, :], lhsT=xq[t][0][:, m].bitcast(FP8X4), lhsT_scale=xq[t][1][:, m],
                                    rhs=wq[k][0][:, f].bitcast(FP8X4), rhs_scale=wq[k][1][:, f], start=True, stop=True)
            copy(eng, hgrp[k, t][:, 512 * c : 512 * (c + 1)].rearrange("p (n s) -> p n s", s=PACK), b[:].rearrange("p s n -> p n s"))

        def h_quant(k, t, lo=0, hi=512):
            quantise(hq[k, t], hgrp[k, t], lo, hi)

        qq = [quantised(f"q{k}", N) for k in range(K)]
        nmax = [const.tile([P, C], F32, name=f"nmax{k}") for k in range(K)]
        sums = [const.tile([P, C], F32, name=f"sums{k}") for k in range(K)]
        rec = [const.tile([P, C], F32, name=f"rec{k}") for k in range(K)]
        ex = {}
        qb = {}
        qgrp = {}

        mt = {}

        def max0(stage):
            if stage == 0:
                mt["a"] = work.tile([P, C, 256], BF16, name="ma", bufs=1)
                nc.vector.tensor_max(out=mt["a"][:], in0=ed[:, :, 0:256], in1=ed[:, :, 256:512])
            elif stage == 1:
                mt["b"] = work.tile([P, C, 128], BF16, name="mb", bufs=1)
                nc.vector.tensor_max(out=mt["b"][:], in0=mt["a"][:, :, 0:128], in1=mt["a"][:, :, 128:256])
            else:
                nc.vector.tensor_reduce(out=nmax[0][:], in_=mt["b"][:], axis=AX.X, op=ALU.max, negate=True)

        def max1(stage):
            if stage == 0:
                mt["c"] = work.tile([P, 2, N], BF16, name="mc", bufs=1)
                nc.vector.tensor_max(out=mt["c"][:], in0=ed[:, 0:2, :], in1=ed[:, 2:4, :])
            elif stage == 1:
                mt["d"] = work.tile([P, N], BF16, name="md", bufs=1)
                nc.vector.tensor_max(out=mt["d"][:], in0=mt["c"][:, 0, :], in1=mt["c"][:, 1, :])
            elif stage == 2:
                mt["e"] = ps_t.tile([P, C, P], BF16, name="t_bank")
                for c in range(C):
                    nc.tensor.transpose(mt["e"][:, c, :], mt["d"][:, P * c : P * (c + 1)], id_b[:])
            else:
                nc.vector.tensor_reduce(out=nmax[1][:], in_=mt["e"][:], axis=AX.X, op=ALU.max, negate=True)

        def exp_row(k, r, src):
            if k not in ex:
                ex[k] = work.tile([P, C, N], F32, name="ex", bufs=3)
            nc.scalar.activation(out=ex[k][:, r, :].rearrange("a (u p e) -> a u p e", u=2, e=2), in_=src.rearrange("a (p u e) -> a u p e", u=2, e=2), func=ACT.Exp, bias=nmax[k][:, r : r + 1], accum_out=sums[k][:, r : r + 1])

        def exp0(r):
            exp_row(0, r, ed[:, r, :])

        ebank = {}

        def p1_turn(half):
            ebank[half] = ps_t.tile([P, 2, N], BF16, name="t_bank")
            for i in range(2):
                r = 2 * half + i
                for c in range(C):
                    nc.tensor.transpose(ebank[half][:, i, P * c : P * (c + 1)], ed[:, c, P * r : P * (r + 1)], id_b[:])

        def exp1(r):
            exp_row(1, r, ebank[r // 2][:, r % 2, :])

        eq = [quantised(f"eq{i}", N) for i in range(2)]
        egrp = {}

        def e_turn(i, half, eng):
            if i not in egrp:
                egrp[i] = work.tile([P, 4 * N], BF16, name="egrp", align_bytes=64)
            turn(es[i], egrp[i], half, eng)

        def e_quant(i):
            quantise(eq[i], egrp[i])

        lg = const.tile([P, C, N], F32, name="lg")
        pmax = const.tile([P, C], F32, name="pmax")

        def logits(r):
            b = ps_t.tile([P, N], F32, name="t_bank")
            m = slice(P * r, P * (r + 1))
            nc.tensor.matmul_mx(out=b[:], lhsT=eq[0][0][:, m].bitcast(FP8X4), lhsT_scale=eq[0][1][:, m],
                                rhs=eq[1][0][:].bitcast(FP8X4), rhs_scale=eq[1][1][:], start=True, stop=True)
            nc.vector.tensor_scalar(out=lg[:, r, :], in0=b[:], scalar1=0.0, scalar2=0.0, op0=ALU.max, op1=ALU.max, accum_out=pmax[:, r : r + 1])

        def negate2():
            nc.scalar.mul(out=nmax[2][:], in_=pmax[:], mul=-1.0)

        def exp2(r):
            exp_row(2, r, lg[:, r, :])

        def recip(k):
            nc.vector.reciprocal(out=rec[k][:], in_=sums[k][:])

        def scale_q(k, r):
            if k not in qb:
                qb[k] = work.tile([P, C, N], BF16, name="qb")
            nc.vector.scalar_tensor_tensor(out=qb[k][:, r, :], in0=ex[k][:, r, :], scalar=rec[k][:, r : r + 1], in1=gb[:, N * k : N * (k + 1)], op0=ALU.mult, op1=ALU.mult)

        def q_turn(k, half, eng):
            if k not in qgrp:
                qgrp[k] = work.tile([P, 4 * N], BF16, name="qgrp", align_bytes=64)
            turn(qb[k], qgrp[k], half, eng, sorted_words=True)

        def q_quant(k):
            quantise(qq[k], qgrp[k])

        zb = {}
        zo = {}

        def z_mm(t, r, ks, lo=0, hi=F):
            if (t, r, lo) not in zb:
                zb[t, r, lo] = ps_z.tile([P, hi - lo], F32, name="z_bank")
            m = slice(P * r, P * (r + 1))
            for k in ks:
                nc.tensor.matmul_mx(out=zb[t, r, lo][:], lhsT=qq[k][0][:, m].bitcast(FP8X4), lhsT_scale=qq[k][1][:, m],
                                    rhs=hq[k, t][0][:, lo:hi].bitcast(FP8X4), rhs_scale=hq[k, t][1][:, lo:hi], start=k == 0, stop=k == K - 1)

        def z_add(t, r, lo=0, hi=F):
            zo[t, r, lo] = work.tile([P, hi - lo], F32, name="z_sum", bufs=4)
            nc.vector.tensor_tensor(out=zo[t, r, lo][:], in0=zb[t, r, lo][:], in1=bias_bc[:, lo:hi], op=ALU.add)

        def z_out(t, r, eng, lo=0, hi=F):
            o = work.tile([P, hi - lo], F32, name="z_out", bufs=6)
            if eng == "A":
                nc.scalar.activation(out=o[:], in_=zo[t, r, lo][:], func=ACT.Relu)
            else:
                nc.vector.tensor_scalar_max(out=o[:], in0=zo[t, r, lo][:], scalar1=0.0)
            nc.sync.dma_start(out=out[t, P * r : P * (r + 1), lo:hi], in_=o[:])

        widen(0, 3, "A")
        g_mm()
        widen(0, 0, "V")
        widen(0, 1, "V")
        g_copy(0)
        widen(0, 2, "V")
        widen(1, 2, "V")
        w_inter(0)
        g_copy(1)
        widen(1, 3, "V")
        widen(1, 0, "A")
        w_quant(0)
        x_turn(0, 1, "A")
        x_turn(0, 0, "A")
        widen(1, 1, "A")
        x_turn(1, 0, "A")
        x_turn(1, 1, "A")
        x_quant(0)
        w_inter(1)
        widen(2, 1, "V")
        widen(2, 2, "A")
        x_quant(1)
        max0(0)
        max1(0)
        widen(2, 0, "V")
        h_unit(0, 0, 0, "A")
        max0(1)
        h_unit(0, 0, 1, "A")
        e_turn(0, 0, "A")
        h_unit(0, 0, 2, "A")
        max1(1)
        h_unit(0, 0, 3, "A")
        e_turn(1, 1, "A")
        e_turn(1, 0, "A")
        w_quant(1)
        h_unit(0, 1, 0, "A")
        widen(2, 3, "V")
        max0(2)
        h_unit(0, 1, 1, "V")
        exp0(2)
        exp0(1)
        e_turn(0, 1, "V")
        max1(2)
        h_unit(0, 1, 2, "A")
        exp0(0)
        max1(3)
        h_unit(0, 1, 3, "V")
        e_quant(0)
        p1_turn(0)
        e_quant(1)
        exp1(1)
        h_unit(1, 0, 0, "V")
        exp1(0)
        p1_turn(1)
        exp1(3)
        exp1(2)
        h_unit(1, 0, 1, "V")
        h_unit(1, 0, 2, "A")
        w_inter(2)
        logits(2)
        h_unit(1, 0, 3, "A")
        logits(3)
        exp0(3)
        h_unit(1, 1, 0, "A")
        h_unit(1, 1, 1, "A")
        recip(1)
        x_turn(2, 1, "A")
        h_unit(1, 1, 2, "A")
        x_turn(3, 0, "A")
        h_quant(1, 0)
        h_unit(1, 1, 3, "A")
        recip(0)
        w_quant(2)
        h_quant(0, 0)
        scale_q(0, 1)
        scale_q(1, 3)
        logits(0)
        h_quant(0, 1)
        scale_q(0, 0)
        scale_q(1, 2)
        h_unit(2, 0, 0, "A")
        x_turn(2, 0, "A")
        h_unit(2, 0, 1, "A")
        h_unit(2, 0, 2, "A")
        x_turn(3, 1, "A")
        logits(1)
        h_unit(2, 0, 3, "A")
        negate2()
        scale_q(1, 1)
        h_unit(2, 1, 0, "A")
        q_turn(1, 1, "A")
        scale_q(0, 2)
        q_turn(0, 0, "A")
        scale_q(0, 3)
        h_unit(2, 1, 1, "A")
        scale_q(1, 0)
        x_quant(2)
        h_unit(2, 1, 2, "V")
        exp2(1)
        exp2(3)
        h_unit(2, 1, 3, "V")
        q_turn(0, 1, "V")
        exp2(2)
        q_turn(1, 0, "A")
        h_unit(2, 2, 0, "V")
        q_quant(0)
        h_unit(2, 2, 1, "A")
        exp2(0)
        q_quant(1)
        h_unit(2, 2, 2, "A")
        h_unit(2, 2, 3, "A")
        recip(2)
        z_mm(0, 2, (0, 1))
        h_quant(1, 1)
        h_unit(1, 2, 0, "A")
        h_unit(1, 2, 1, "A")
        scale_q(2, 1)
        scale_q(2, 0)
        z_mm(1, 3, (0, 1))
        scale_q(2, 3)
        h_unit(1, 2, 2, "A")
        scale_q(2, 2)
        h_unit(1, 2, 3, "A")
        q_turn(2, 0, "A")
        h_quant(2, 0)
        q_turn(2, 1, "V")
        q_quant(2)
        h_unit(0, 2, 0, "A")
        h_unit(0, 2, 1, "A")
        z_mm(1, 1, (0, 1))
        z_mm(0, 3, (0, 1))
        h_unit(0, 2, 2, "A")
        z_mm(0, 2, (2,))
        h_quant(2, 1)
        x_quant(3)
        h_unit(0, 2, 3, "A")
        z_mm(1, 3, (2,))
        z_add(0, 2)
        z_mm(1, 1, (2,))
        h_unit(0, 3, 0, "A")
        z_mm(0, 3, (2,))
        z_add(1, 3)
        h_quant(2, 2)
        z_add(1, 1)
        h_unit(0, 3, 1, "A")
        h_quant(0, 2)
        z_mm(0, 0, (0, 1))
        h_unit(0, 3, 2, "A")
        z_mm(0, 0, (2,))
        h_unit(0, 3, 3, "A")
        z_out(0, 2, "V")
        z_out(1, 3, "V")
        z_mm(0, 1, (0, 1))
        h_unit(1, 3, 0, "A")
        z_mm(0, 1, (2,))
        z_add(0, 0)
        h_unit(1, 3, 1, "A")
        z_mm(1, 0, (0, 1))
        z_add(0, 3)
        z_out(1, 1, "V")
        z_out(0, 0, "A")
        h_unit(1, 3, 2, "A")
        z_mm(1, 0, (2,))
        h_quant(1, 2)
        h_unit(1, 3, 3, "A")
        h_quant(0, 3)
        z_mm(2, 0, (0, 1))
        z_add(1, 0)
        z_out(1, 0, "A")
        z_mm(2, 0, (2,))
        h_unit(2, 3, 0, "A")
        z_mm(2, 3, (0, 1))
        z_out(0, 3, "V")
        z_add(0, 1)
        h_unit(2, 3, 1, "A")
        z_mm(2, 2, (0, 1))
        z_add(2, 0)
        z_out(0, 1, "V")
        h_quant(1, 3)
        z_mm(2, 2, (2,))
        z_out(2, 0, "V")
        z_add(2, 2)
        h_unit(2, 3, 2, "A")
        h_unit(2, 3, 3, "A")
        z_mm(2, 3, (2,))
        z_mm(2, 1, (0, 1))
        z_mm(1, 2, (0, 1))
        z_mm(2, 1, (2,))
        z_add(2, 3)
        z_out(2, 2, "A")
        h_quant(2, 3)
        z_mm(1, 2, (2,))
        z_out(2, 3, "A")
        z_mm(3, 0, (0, 1))
        z_add(2, 1)
        z_mm(3, 0, (2,))
        z_mm(3, 2, (0, 1))
        z_mm(3, 2, (2,))
        z_mm(3, 1, (0, 1))
        z_add(1, 2)
        z_out(2, 1, "A")
        z_mm(3, 1, (2,))
        z_mm(3, 3, (0, 1), 0, 256)
        z_add(3, 0)
        z_out(1, 2, "V")
        z_mm(3, 3, (2,), 0, 256)
        z_add(3, 2)
        z_add(3, 1)
        z_add(3, 3, 0, 256)
        z_out(3, 0, "A")
        z_out(3, 2, "A")
        z_mm(3, 3, (0, 1), 256, 512)
        z_out(3, 1, "V")
        z_mm(3, 3, (2,), 256, 512)
        z_add(3, 3, 256, 512)
        z_out(3, 3, "V", 0, 256)
        z_out(3, 3, "V", 256, 512)
